import numpy as np
import ml_dtypes


def mxq(x, axis, fmt="e4m3"):
    dtype, down = {"e4m3": (ml_dtypes.float8_e4m3fn, 7), "e5m2": (ml_dtypes.float8_e5m2, 14)}[fmt]
    v = np.moveaxis(np.asarray(x, np.float32).astype(ml_dtypes.bfloat16).astype(np.float64), axis, -1)
    blocks = v.reshape(v.shape[:-1] + (-1, 32))
    amax = np.abs(blocks).max(-1, keepdims=True)
    byte = np.maximum(np.where(amax > 0, np.frexp(amax)[1] - 1 + 127, 0) - down, 1)
    scale = np.exp2(byte - 127.0)
    codes = (blocks / scale).astype(np.float32).astype(dtype).astype(np.float64)
    return np.moveaxis((codes * scale).reshape(v.shape), -1, axis)


WIDE = False


def mx_kscale(k):
    if not WIDE:
        return np.ones(k)
    levels = np.array([10, -10, 5, -5, 0])
    if k % 512:
        return np.exp2(np.random.permutation(np.resize(levels, k // 32))).repeat(32)
    a = np.empty((k // 512, 16))
    for p in range(k // 512):
        a[p, :8] = np.random.permutation(np.resize(levels, 8))
        for g in range(8):
            far = levels[np.abs(levels - a[p, g]) >= 10]
            a[p, g + 8] = far[np.random.randint(len(far))]
    return np.exp2(a.ravel()).repeat(32)


def f64(x):
    return np.asarray(x).astype(np.float64)


def striped(idx):
    return np.tile(idx.reshape(-1, 16).T, (8, 1)).astype(np.uint16)


def unstriped(offs):
    return offs[:16].T.reshape(-1).astype(np.int64)


E2M1 = np.array([0.0, 0.5, 1.0, 1.5, 2.0, 3.0, 4.0, 6.0, -0.0, -0.5, -1.0, -1.5, -2.0, -3.0, -4.0, -6.0])


def pack_weight(w, fmt):
    k, n = w.shape
    w = f64(np.asarray(w, np.float32).astype(ml_dtypes.bfloat16)).reshape(k // 32, 32, n)
    amax = np.abs(w).max(1)
    if fmt == "e4m3":
        byte = np.frexp(amax)[1] - 1 + 127 - 7
    else:
        mant, ex = np.frexp(amax / 6.0)
        byte = np.where(mant > 0.5, ex, ex - 1) + 127
    byte = np.clip(np.where(amax > 0, byte, 1), 1, 254)
    scaled = (w * np.exp2(127.0 - byte)[:, None, :]).reshape(k, n).astype(np.float32)
    by_word = np.ascontiguousarray(scaled.reshape(k // 512, 128, 4, n).transpose(0, 1, 3, 2))
    if fmt == "e4m3":
        words = by_word.astype(ml_dtypes.float8_e4m3fn).view(np.uint8)
    else:
        c = by_word.astype(ml_dtypes.float4_e2m1fn).view(np.uint8) & 0xF
        words = (c[..., 0::2] | (c[..., 1::2] << 4)).reshape(k // 512, 128, 2 * n)
    return np.ascontiguousarray(words), np.ascontiguousarray(byte.astype(np.uint8).reshape(k // 512, 16, n))


def unpack_weight(words, scales, fmt):
    g, _, n = scales.shape
    words = np.ascontiguousarray(words).reshape(g, 128, n, -1)
    if fmt == "e4m3":
        vals = words.view(ml_dtypes.float8_e4m3fn).astype(np.float64)
    else:
        nib = np.empty((g, 128, n, 4), np.uint8)
        nib[..., 0::2] = words & 0xF
        nib[..., 1::2] = words >> 4
        vals = E2M1[nib]
    vals = vals * np.repeat(np.exp2(scales.astype(np.float64) - 127.0), 8, axis=1)[..., None]
    return vals.transpose(0, 1, 3, 2).reshape(g * 512, n)


def pack_table4(v):
    words, scales = pack_weight(v, "e2m1")
    g, t = words.shape[0] // 2, v.shape[1]
    words = words.reshape(g, 2, 128, t, 2).transpose(0, 2, 3, 1, 4)
    return np.concatenate([words.reshape(g, -1), scales.reshape(g, -1)], axis=1)


def unpack_table4(tab):
    g, t = tab.shape[0], tab.shape[1] // 544
    words = tab[:, :512 * t].reshape(g, 128, t, 2, 2).transpose(0, 3, 1, 2, 4).reshape(2 * g, 128, 2 * t)
    return unpack_weight(words, tab[:, 512 * t:].reshape(2 * g, 16, t), "e2m1")


def gelu(v):
    return 0.5 * v * (1.0 + np.tanh(np.sqrt(2.0 / np.pi) * (v + 0.044715 * v**3)))


K, M, T, S = 3072, 1024, 2048, 1024


def setup_inputs():
    n = np.random.standard_normal
    s = mx_kscale(K)[:, None]
    return {
        "tab": pack_table4(n((K, T)) * s),
        "w": (n((K, M)) / np.sqrt(K) / s).astype(np.float32),
        "b": (0.3 * n(1024)).astype(np.float32),
        "offs": striped(np.random.permutation(T)[:S]),
    }


def reference(tab, w, b, offs):
    tab_ = unpack_table4(tab)[:, unstriped(offs)]
    w_ = mxq(f64(w), 0, "e4m3")
    y = tab_.T @ w_
    return gelu(y + f64(b)[None, :])

@@ -1,0 +1,161 @@
+from contextlib import ExitStack
+
+import concourse.mybir as mybir
+from concourse.masks import make_identity
+
+K, M, T, S = 3072, 1024, 2048, 1024
+FLOPS = 2 * K * M * S
+
+F32 = mybir.dt.float32
+BF16 = mybir.dt.bfloat16
+I32 = mybir.dt.int32
+U32 = mybir.dt.uint32
+U16 = mybir.dt.uint16
+U8 = mybir.dt.uint8
+FP8X4 = mybir.dt.float8_e4m3fn_x4
+FP4X4 = mybir.dt.float4_e2m1fn_x4
+GELU = mybir.ActivationFunctionType.Gelu_apprx_tanh
+ADD = mybir.AluOpType.add
+
+P = 128
+PAIRS = K // 1024
+NW = 512
+HALVES = M // NW
+TILES = S // P
+WORD_BYTES = 512 * T
+SPLIT = (384, 256)
+
+
+def tile_list_tab4_tm_gelu_kernel(tc, tab, w, b, offs, out):
+    nc = tc.nc
+    with ExitStack() as ctx:
+        keep = ctx.enter_context(tc.tile_pool(name="keep", bufs=1))
+        wpool = ctx.enter_context(tc.tile_pool(name="wpool", bufs=12))
+        gpool = ctx.enter_context(tc.tile_pool(name="gpool", bufs=2))
+        xpool = ctx.enter_context(tc.tile_pool(name="xpool", bufs=4))
+        cpool = ctx.enter_context(tc.tile_pool(name="cpool", bufs=8))
+        ypool = ctx.enter_context(tc.tile_pool(name="ypool", bufs=16))
+        psum = ctx.enter_context(tc.psum_pool(name="psum", bufs=8))
+
+        offsets = keep.tile([P, S // 16], U16, name="offsets")
+        words = [keep.tile([P, T], I32, name=f"words{m}") for m in range(PAIRS)]
+        sc = keep.tile([P, PAIRS * T], U8, name="sc", align_bytes=64)
+        scg = keep.tile([P, PAIRS * S], U8, name="scg", align_bytes=64)
+        sco = keep.tile([P, PAIRS * S], U8, name="sco", align_bytes=64)
+        brow = keep.tile([P, P], F32, name="brow")
+        ident = keep.tile([P, P], F32, name="ident")
+        bcol = keep.tile([P, M // P], F32, name="bcol")
+        bias = keep.tile([P, M], F32, name="bias")
+        warm = keep.tile([P, 1], F32, name="warm")
+
+        nc.vector.memset(sc[:].bitcast(I32), 0)
+        nc.gpsimd.memset(brow[:], 0.0)
+        nc.gpsimd.memset(sco[:].bitcast(I32), 0)
+        nc.gpsimd.memset(warm[:], 0.0)
+        make_identity(nc, ident[:])
+        nc.scalar.activation(warm[:], warm[:], GELU)
+
+        def load_words(m):
+            nc.sync.dma_start(words[m][:], tab[m, 0:WORD_BYTES].bitcast(I32).rearrange("(p t) -> p t", p=P))
+
+        chunks = {}
+
+        def load_w(half, a):
+            raw = wpool.tile([P, 4, NW], F32, name="raw")
+            nc.sync.dma_start(raw[:], w[512 * a : 512 * (a + 1), NW * half : NW * (half + 1)].rearrange("(p j) n -> p j n", j=4))
+            chunks[half, a] = raw
+
+        planes = tab[:, WORD_BYTES : WORD_BYTES + 32 * T].bitcast(I32).rearrange("m (h q r t) -> h q r m t", h=2, q=4, r=4)
+        sc_words = sc[:].bitcast(I32).rearrange("p (m t) -> p m t", m=PAIRS)
+        for q in range(4):
+            nc.sync.dma_start(sc_words[32 * q : 32 * q + 4], planes[0, q])
+        odd = tab[:, WORD_BYTES + 16 * T : WORD_BYTES + 32 * T].bitcast(I32).rearrange("m (s t) -> s m t", s=16)
+        nc.sync.dma_start(sc_words[4:20], odd)
+        nc.sync.dma_start(offsets[:], offs)
+        load_words(0)
+        nc.sync.dma_start(brow[0:8, :], b.rearrange("(m n) -> m n", m=8))
+        load_w(0, 0)
+        load_w(0, 1)
+        load_words(1)
+        load_w(0, 2)
+        load_w(0, 3)
+        load_words(2)
+        load_w(0, 4)
+        load_w(0, 5)
+        for a in range(6):
+            load_w(1, a)
+
+        tp = psum.tile([P, NW], F32, name="acc")
+        nc.tensor.transpose(tp[:, 0:P], brow[:], ident[:])
+        nc.scalar.copy(bcol[:], tp[:, 0:8])
+        for half in range(HALVES):
+            bp = psum.tile([P, NW], F32, name="acc")
+            for q in range(4):
+                nc.tensor.transpose(bp[:, P * q : P * (q + 1)], bcol[:, 4 * half + q : 4 * half + q + 1].to_broadcast([P, P]), ident[:])
+            nc.scalar.copy(bias[:, NW * half : NW * (half + 1)], bp[:])
+
+        parted = []
+
+        def gather_scales(m):
+            nc.vector.tensor_copy(scg[:, S * m : S * (m + 1)], sc[:, T * m : T * (m + 1)].indirect(offsets[:]))
+
+        def move_odd(queue, m0, m1):
+            for q in range(4):
+                queue.dma_start(
+                    sco[32 * q : 32 * q + 4, S * m0 : S * m1].bitcast(I32),
+                    scg[4 + 4 * q : 8 + 4 * q, S * m0 : S * m1].bitcast(I32),
+                )
+
+        def gather(m):
+            got = gpool.tile([P, S], U32, name="got")
+            nc.vector.tensor_copy(got[:], words[m][:].bitcast(U32).indirect(offsets[:]))
+            pt = keep.tile([P, 4 * S], U8, name=f"parted{m}", align_bytes=64)
+            nc.vector.tensor_copy(
+                pt[:].bitcast(U16).rearrange("p (h t) -> p h t", h=2),
+                got[:].bitcast(U16).rearrange("p (t h) -> p h t", h=2),
+            )
+            parted.append(pt)
+
+        def quantize(half, a):
+            raw = chunks[half, a]
+            x = xpool.tile([P, 4 * NW], BF16, name="x", align_bytes=64)
+            for engine, lo, hi in ((nc.scalar.copy, 0, SPLIT[half]), (nc.vector.tensor_copy, SPLIT[half], NW)):
+                engine(
+                    x[:, 4 * lo : 4 * hi].rearrange("p (c i t) -> p c t i", i=4, t=4),
+                    raw[:, :, lo:hi].rearrange("p t (c i) -> p c t i", i=4),
+                )
+            codes = cpool.tile([P, NW], U32, name="codes", align_bytes=64)
+            scales = cpool.tile([P, NW], U8, name="scales", align_bytes=64)
+            nc.vector.quantize_mx(out=codes[:].bitcast(FP8X4), scales=scales[:], in_=x[:])
+            return codes, scales
+
+        for half in range(HALVES):
+            acc = [psum.tile([P, NW], F32, name="acc") for j in range(TILES)]
+            for a in range(2 * PAIRS):
+                m, h = divmod(a, 2)
+                if half == 0 and a == 0:
+                    gather_scales(0)
+                    move_odd(nc.scalar, 0, 1)
+                    gather(0)
+                    gather_scales(1)
+                    gather_scales(2)
+                    move_odd(nc.scalar, 1, 3)
+                elif half == 0 and h == 0:
+                    gather(m)
+                codes, scales = quantize(half, a)
+                plane = scg if h == 0 else sco
+                for j in range(TILES):
+                    nc.tensor.matmul_mx(
+                        out=acc[j][:],
+                        lhsT=parted[m][:, 2 * S * h + 2 * P * j : 2 * S * h + 2 * P * (j + 1)].bitcast(FP4X4),
+                        lhsT_scale=plane[:, S * m + P * j : S * m + P * (j + 1)],
+                        rhs=codes[:].bitcast(FP8X4),
+                        rhs_scale=scales[:],
+                        start=(a == 0),
+                        stop=(a == 2 * PAIRS - 1),
+                    )
+            for j in range(TILES):
+                y = ypool.tile([P, NW], F32, name="y")
+                nc.vector.tensor_tensor(y[:], acc[j][:], bias[:, NW * half : NW * (half + 1)], ADD)
+                nc.scalar.activation(y[:], y[:], GELU)
+                nc.sync.dma_start(out[P * j : P * (j + 1), NW * half : NW * (half + 1)], y[:])

@@ -23,14 +23,17 @@ NW = 512
 HALVES = M // NW
 TILES = S // P
 WORD_BYTES = 512 * T
-SPLIT = (384, 256)
+SCALAR_COLUMNS = [512] * 6 + [256] * 4 + [192] * 2
+
+
+AHEAD = 4
 
 
 def tile_list_tab4_tm_gelu_kernel(tc, tab, w, b, offs, out):
     nc = tc.nc
     with ExitStack() as ctx:
         keep = ctx.enter_context(tc.tile_pool(name="keep", bufs=1))
-        wpool = ctx.enter_context(tc.tile_pool(name="wpool", bufs=12))
+        wpool = ctx.enter_context(tc.tile_pool(name="wpool", bufs=4))
         gpool = ctx.enter_context(tc.tile_pool(name="gpool", bufs=2))
         xpool = ctx.enter_context(tc.tile_pool(name="xpool", bufs=4))
         cpool = ctx.enter_context(tc.tile_pool(name="cpool", bufs=8))
@@ -48,42 +51,49 @@ def tile_list_tab4_tm_gelu_kernel(tc, tab, w, b, offs, out):
         bias = keep.tile([P, M], F32, name="bias")
         warm = keep.tile([P, 1], F32, name="warm")
 
+        chunk_list = [(half, a) for half in range(HALVES) for a in range(2 * PAIRS)]
+        raws = []
+
+        def new_raw():
+            raw = wpool.tile([P, 4, NW], F32, name="raw")
+            raws.append(raw)
+            return raw
+
         nc.vector.memset(sc[:].bitcast(I32), 0)
+        first = [new_raw() for i in range(4)]
+        for m in range(PAIRS):
+            nc.vector.memset(words[m][:, 0:1], 0)
+        for raw in first:
+            nc.vector.memset(raw[:, 0, 0:1], 0.0)
         nc.gpsimd.memset(brow[:], 0.0)
-        nc.gpsimd.memset(sco[:].bitcast(I32), 0)
         nc.gpsimd.memset(warm[:], 0.0)
         make_identity(nc, ident[:])
+        nc.gpsimd.memset(sco[:].bitcast(I32), 0)
         nc.scalar.activation(warm[:], warm[:], GELU)
 
         def load_words(m):
             nc.sync.dma_start(words[m][:], tab[m, 0:WORD_BYTES].bitcast(I32).rearrange("(p t) -> p t", p=P))
 
-        chunks = {}
-
-        def load_w(half, a):
-            raw = wpool.tile([P, 4, NW], F32, name="raw")
+        def load_w(i):
+            half, a = chunk_list[i]
+            raw = raws[i] if i < 4 else new_raw()
             nc.sync.dma_start(raw[:], w[512 * a : 512 * (a + 1), NW * half : NW * (half + 1)].rearrange("(p j) n -> p j n", j=4))
-            chunks[half, a] = raw
 
+        nc.sync.dma_start(offsets[:], offs)
+        nc.sync.dma_start(brow[0:8, :], b.rearrange("(m n) -> m n", m=8))
         planes = tab[:, WORD_BYTES : WORD_BYTES + 32 * T].bitcast(I32).rearrange("m (h q r t) -> h q r m t", h=2, q=4, r=4)
         sc_words = sc[:].bitcast(I32).rearrange("p (m t) -> p m t", m=PAIRS)
         for q in range(4):
             nc.sync.dma_start(sc_words[32 * q : 32 * q + 4], planes[0, q])
         odd = tab[:, WORD_BYTES + 16 * T : WORD_BYTES + 32 * T].bitcast(I32).rearrange("m (s t) -> s m t", s=16)
         nc.sync.dma_start(sc_words[4:20], odd)
-        nc.sync.dma_start(offsets[:], offs)
         load_words(0)
-        nc.sync.dma_start(brow[0:8, :], b.rearrange("(m n) -> m n", m=8))
-        load_w(0, 0)
-        load_w(0, 1)
+        load_w(0)
         load_words(1)
-        load_w(0, 2)
-        load_w(0, 3)
+        load_w(1)
         load_words(2)
-        load_w(0, 4)
-        load_w(0, 5)
-        for a in range(6):
-            load_w(1, a)
+        load_w(2)
+        load_w(3)
 
         tp = psum.tile([P, NW], F32, name="acc")
         nc.tensor.transpose(tp[:, 0:P], brow[:], ident[:])
@@ -94,68 +104,75 @@ def tile_list_tab4_tm_gelu_kernel(tc, tab, w, b, offs, out):
                 nc.tensor.transpose(bp[:, P * q : P * (q + 1)], bcol[:, 4 * half + q : 4 * half + q + 1].to_broadcast([P, P]), ident[:])
             nc.scalar.copy(bias[:, NW * half : NW * (half + 1)], bp[:])
 
-        parted = []
-
-        def gather_scales(m):
+        for m in range(PAIRS):
             nc.vector.tensor_copy(scg[:, S * m : S * (m + 1)], sc[:, T * m : T * (m + 1)].indirect(offsets[:]))
+        for q in range(4):
+            nc.sync.dma_start(sco[32 * q : 32 * q + 4, :].bitcast(I32), scg[4 + 4 * q : 8 + 4 * q, :].bitcast(I32))
 
-        def move_odd(queue, m0, m1):
-            for q in range(4):
-                queue.dma_start(
-                    sco[32 * q : 32 * q + 4, S * m0 : S * m1].bitcast(I32),
-                    scg[4 + 4 * q : 8 + 4 * q, S * m0 : S * m1].bitcast(I32),
-                )
+        parted = []
 
         def gather(m):
             got = gpool.tile([P, S], U32, name="got")
             nc.vector.tensor_copy(got[:], words[m][:].bitcast(U32).indirect(offsets[:]))
-            pt = keep.tile([P, 4 * S], U8, name=f"parted{m}", align_bytes=64)
-            nc.vector.tensor_copy(
-                pt[:].bitcast(U16).rearrange("p (h t) -> p h t", h=2),
-                got[:].bitcast(U16).rearrange("p (t h) -> p h t", h=2),
-            )
-            parted.append(pt)
+            for h in range(2):
+                pt = keep.tile([P, 2 * S], U8, name=f"parted{2 * m + h}", align_bytes=64)
+                nc.vector.tensor_copy(pt[:].bitcast(U16), got[:].bitcast(U16).rearrange("p (t h) -> p h t", h=2)[:, h, :])
+                parted.append(pt)
 
-        def quantize(half, a):
-            raw = chunks[half, a]
+        quantized = []
+
+        def quantize(i):
+            raw = raws[i]
             x = xpool.tile([P, 4 * NW], BF16, name="x", align_bytes=64)
-            for engine, lo, hi in ((nc.scalar.copy, 0, SPLIT[half]), (nc.vector.tensor_copy, SPLIT[half], NW)):
-                engine(
-                    x[:, 4 * lo : 4 * hi].rearrange("p (c i t) -> p c t i", i=4, t=4),
-                    raw[:, :, lo:hi].rearrange("p t (c i) -> p c t i", i=4),
-                )
+            cut = SCALAR_COLUMNS[i]
+            for engine, lo, hi in ((nc.scalar.copy, 0, cut), (nc.vector.tensor_copy, cut, NW)):
+                if lo < hi:
+                    engine(
+                        x[:, 4 * lo : 4 * hi].rearrange("p (c i t) -> p c t i", i=4, t=4),
+                        raw[:, :, lo:hi].rearrange("p t (c i) -> p c t i", i=4),
+                    )
             codes = cpool.tile([P, NW], U32, name="codes", align_bytes=64)
             scales = cpool.tile([P, NW], U8, name="scales", align_bytes=64)
             nc.vector.quantize_mx(out=codes[:].bitcast(FP8X4), scales=scales[:], in_=x[:])
-            return codes, scales
+            quantized.append((codes, scales))
+            if i + 4 < len(chunk_list):
+                load_w(i + 4)
 
-        for half in range(HALVES):
-            acc = [psum.tile([P, NW], F32, name="acc") for j in range(TILES)]
-            for a in range(2 * PAIRS):
-                m, h = divmod(a, 2)
-                if half == 0 and a == 0:
-                    gather_scales(0)
-                    move_odd(nc.scalar, 0, 1)
-                    gather(0)
-                    gather_scales(1)
-                    gather_scales(2)
-                    move_odd(nc.scalar, 1, 3)
-                elif half == 0 and h == 0:
-                    gather(m)
-                codes, scales = quantize(half, a)
-                plane = scg if h == 0 else sco
-                for j in range(TILES):
-                    nc.tensor.matmul_mx(
-                        out=acc[j][:],
-                        lhsT=parted[m][:, 2 * S * h + 2 * P * j : 2 * S * h + 2 * P * (j + 1)].bitcast(FP4X4),
-                        lhsT_scale=plane[:, S * m + P * j : S * m + P * (j + 1)],
-                        rhs=codes[:].bitcast(FP8X4),
-                        rhs_scale=scales[:],
-                        start=(a == 0),
-                        stop=(a == 2 * PAIRS - 1),
-                    )
+        def multiply(i, acc):
+            half, a = chunk_list[i]
+            m, h = divmod(a, 2)
+            codes, scales = quantized[i]
+            plane = (scg, sco)[h]
+            for j in range(TILES):
+                nc.tensor.matmul_mx(
+                    out=acc[j][:],
+                    lhsT=parted[a][:, 2 * P * j : 2 * P * (j + 1)].bitcast(FP4X4),
+                    lhsT_scale=plane[:, S * m + P * j : S * m + P * (j + 1)],
+                    rhs=codes[:].bitcast(FP8X4),
+                    rhs_scale=scales[:],
+                    start=(a == 0),
+                    stop=(a == 2 * PAIRS - 1),
+                )
+
+        def finish(half, acc):
             for j in range(TILES):
                 y = ypool.tile([P, NW], F32, name="y")
                 nc.vector.tensor_tensor(y[:], acc[j][:], bias[:, NW * half : NW * (half + 1)], ADD)
                 nc.scalar.activation(y[:], y[:], GELU)
                 nc.sync.dma_start(out[P * j : P * (j + 1), NW * half : NW * (half + 1)], y[:])
+
+        acc = [psum.tile([P, NW], F32, name="acc") for j in range(TILES)]
+        for a in range(6):
+            if a % 2 == 0:
+                gather(a // 2)
+            quantize(a)
+            multiply(a, acc)
+        for i in range(6, 6 + AHEAD):
+            quantize(i)
+        finish(0, acc)
+        acc = [psum.tile([P, NW], F32, name="acc") for j in range(TILES)]
+        for i in range(6, 12):
+            if i >= 6 + AHEAD:
+                quantize(i)
+            multiply(i, acc)
+        finish(1, acc)

@@ -23,10 +23,7 @@ NW = 512
 HALVES = M // NW
 TILES = S // P
 WORD_BYTES = 512 * T
-SCALAR_COLUMNS = [512] * 6 + [256] * 4 + [192] * 2
-
-
-AHEAD = 4
+SCALAR_COLUMNS = [512] * 6 + [256] * 6
 
 
 def tile_list_tab4_tm_gelu_kernel(tc, tab, w, b, offs, out):
@@ -61,7 +58,7 @@ def tile_list_tab4_tm_gelu_kernel(tc, tab, w, b, offs, out):
 
         nc.vector.memset(sc[:].bitcast(I32), 0)
         first = [new_raw() for i in range(4)]
-        for m in range(PAIRS):
+        for m in range(1, PAIRS):
             nc.vector.memset(words[m][:, 0:1], 0)
         for raw in first:
             nc.vector.memset(raw[:, 0, 0:1], 0.0)
@@ -80,6 +77,7 @@ def tile_list_tab4_tm_gelu_kernel(tc, tab, w, b, offs, out):
             nc.sync.dma_start(raw[:], w[512 * a : 512 * (a + 1), NW * half : NW * (half + 1)].rearrange("(p j) n -> p j n", j=4))
 
         nc.sync.dma_start(offsets[:], offs)
+        load_words(0)
         nc.sync.dma_start(brow[0:8, :], b.rearrange("(m n) -> m n", m=8))
         planes = tab[:, WORD_BYTES : WORD_BYTES + 32 * T].bitcast(I32).rearrange("m (h q r t) -> h q r m t", h=2, q=4, r=4)
         sc_words = sc[:].bitcast(I32).rearrange("p (m t) -> p m t", m=PAIRS)
@@ -87,12 +85,11 @@ def tile_list_tab4_tm_gelu_kernel(tc, tab, w, b, offs, out):
             nc.sync.dma_start(sc_words[32 * q : 32 * q + 4], planes[0, q])
         odd = tab[:, WORD_BYTES + 16 * T : WORD_BYTES + 32 * T].bitcast(I32).rearrange("m (s t) -> s m t", s=16)
         nc.sync.dma_start(sc_words[4:20], odd)
-        load_words(0)
         load_w(0)
         load_words(1)
         load_w(1)
-        load_words(2)
         load_w(2)
+        load_words(2)
         load_w(3)
 
         tp = psum.tile([P, NW], F32, name="acc")
@@ -111,13 +108,18 @@ def tile_list_tab4_tm_gelu_kernel(tc, tab, w, b, offs, out):
 
         parted = []
 
+        got_of = {}
+
         def gather(m):
             got = gpool.tile([P, S], U32, name="got")
             nc.vector.tensor_copy(got[:], words[m][:].bitcast(U32).indirect(offsets[:]))
-            for h in range(2):
-                pt = keep.tile([P, 2 * S], U8, name=f"parted{2 * m + h}", align_bytes=64)
-                nc.vector.tensor_copy(pt[:].bitcast(U16), got[:].bitcast(U16).rearrange("p (t h) -> p h t", h=2)[:, h, :])
-                parted.append(pt)
+            got_of[m] = got
+
+        def part(a):
+            m, h = divmod(a, 2)
+            pt = keep.tile([P, 2 * S], U8, name=f"parted{a}", align_bytes=64)
+            nc.vector.tensor_copy(pt[:].bitcast(U16), got_of[m][:].bitcast(U16).rearrange("p (t h) -> p h t", h=2)[:, h, :])
+            parted.append(pt)
 
         quantized = []
 
@@ -138,26 +140,33 @@ def tile_list_tab4_tm_gelu_kernel(tc, tab, w, b, offs, out):
             if i + 4 < len(chunk_list):
                 load_w(i + 4)
 
-        def multiply(i, acc):
-            half, a = chunk_list[i]
-            m, h = divmod(a, 2)
-            codes, scales = quantized[i]
-            plane = (scg, sco)[h]
+        def multiply(chunks, acc):
             for j in range(TILES):
-                nc.tensor.matmul_mx(
-                    out=acc[j][:],
-                    lhsT=parted[a][:, 2 * P * j : 2 * P * (j + 1)].bitcast(FP4X4),
-                    lhsT_scale=plane[:, S * m + P * j : S * m + P * (j + 1)],
-                    rhs=codes[:].bitcast(FP8X4),
-                    rhs_scale=scales[:],
-                    start=(a == 0),
-                    stop=(a == 2 * PAIRS - 1),
-                )
+                for i in chunks:
+                    a = i % 6
+                    m, h = divmod(a, 2)
+                    codes, scales = quantized[i]
+                    plane = (scg, sco)[h]
+                    nc.tensor.matmul_mx(
+                        out=acc[j][:],
+                        lhsT=parted[a][:, 2 * P * j : 2 * P * (j + 1)].bitcast(FP4X4),
+                        lhsT_scale=plane[:, S * m + P * j : S * m + P * (j + 1)],
+                        rhs=codes[:].bitcast(FP8X4),
+                        rhs_scale=scales[:],
+                        start=(a == 0),
+                        stop=(a == 5),
+                    )
 
-        def finish(half, acc):
+        def add_bias(half, acc):
+            ys = []
             for j in range(TILES):
                 y = ypool.tile([P, NW], F32, name="y")
                 nc.vector.tensor_tensor(y[:], acc[j][:], bias[:, NW * half : NW * (half + 1)], ADD)
+                ys.append(y)
+            return ys
+
+        def finish(half, ys):
+            for j, y in enumerate(ys):
                 nc.scalar.activation(y[:], y[:], GELU)
                 nc.sync.dma_start(out[P * j : P * (j + 1), NW * half : NW * (half + 1)], y[:])
 
@@ -165,14 +174,17 @@ def tile_list_tab4_tm_gelu_kernel(tc, tab, w, b, offs, out):
         for a in range(6):
             if a % 2 == 0:
                 gather(a // 2)
+            part(a)
             quantize(a)
-            multiply(a, acc)
-        for i in range(6, 6 + AHEAD):
+            multiply([a], acc)
+        for i in range(6, 8):
             quantize(i)
-        finish(0, acc)
+        ys = add_bias(0, acc)
+        for i in range(8, 12):
+            quantize(i)
+        finish(0, ys)
         acc = [psum.tile([P, NW], F32, name="acc") for j in range(TILES)]
-        for i in range(6, 12):
-            if i >= 6 + AHEAD:
-                quantize(i)
-            multiply(i, acc)
-        finish(1, acc)
+        for i in range(6, 9):
+            multiply([i], acc)
+        multiply([9, 10, 11], acc)
+        finish(1, add_bias(1, acc))

@@ -34,7 +34,8 @@ def tile_list_tab4_tm_gelu_kernel(tc, tab, w, b, offs, out):
         gpool = ctx.enter_context(tc.tile_pool(name="gpool", bufs=2))
         xpool = ctx.enter_context(tc.tile_pool(name="xpool", bufs=4))
         cpool = ctx.enter_context(tc.tile_pool(name="cpool", bufs=8))
-        ypool = ctx.enter_context(tc.tile_pool(name="ypool", bufs=16))
+        ypool = ctx.enter_context(tc.tile_pool(name="ypool", bufs=4))
+        zpool = ctx.enter_context(tc.tile_pool(name="zpool", bufs=9))
         psum = ctx.enter_context(tc.psum_pool(name="psum", bufs=8))
 
         offsets = keep.tile([P, S // 16], U16, name="offsets")
@@ -86,8 +87,8 @@ def tile_list_tab4_tm_gelu_kernel(tc, tab, w, b, offs, out):
         odd = tab[:, WORD_BYTES + 16 * T : WORD_BYTES + 32 * T].bitcast(I32).rearrange("m (s t) -> s m t", s=16)
         nc.sync.dma_start(sc_words[4:20], odd)
         load_w(0)
-        load_words(1)
         load_w(1)
+        load_words(1)
         load_w(2)
         load_words(2)
         load_w(3)
@@ -101,10 +102,15 @@ def tile_list_tab4_tm_gelu_kernel(tc, tab, w, b, offs, out):
                 nc.tensor.transpose(bp[:, P * q : P * (q + 1)], bcol[:, 4 * half + q : 4 * half + q + 1].to_broadcast([P, P]), ident[:])
             nc.scalar.copy(bias[:, NW * half : NW * (half + 1)], bp[:])
 
-        for m in range(PAIRS):
+        def gather_scales(m):
             nc.vector.tensor_copy(scg[:, S * m : S * (m + 1)], sc[:, T * m : T * (m + 1)].indirect(offsets[:]))
-        for q in range(4):
-            nc.sync.dma_start(sco[32 * q : 32 * q + 4, :].bitcast(I32), scg[4 + 4 * q : 8 + 4 * q, :].bitcast(I32))
+
+        def move_odd_planes(m0, m1):
+            for q in range(4):
+                nc.scalar.dma_start(
+                    sco[32 * q : 32 * q + 4, S * m0 : S * m1].bitcast(I32),
+                    scg[4 + 4 * q : 8 + 4 * q, S * m0 : S * m1].bitcast(I32),
+                )
 
         parted = []
 
@@ -165,26 +171,44 @@ def tile_list_tab4_tm_gelu_kernel(tc, tab, w, b, offs, out):
                 ys.append(y)
             return ys
 
-        def finish(half, ys):
-            for j, y in enumerate(ys):
-                nc.scalar.activation(y[:], y[:], GELU)
-                nc.sync.dma_start(out[P * j : P * (j + 1), NW * half : NW * (half + 1)], y[:])
-
         acc = [psum.tile([P, NW], F32, name="acc") for j in range(TILES)]
+        gather(0)
+        gather_scales(0)
+        move_odd_planes(0, 1)
         for a in range(6):
-            if a % 2 == 0:
-                gather(a // 2)
+            if a == 2:
+                gather_scales(1)
+                gather_scales(2)
+                move_odd_planes(1, 3)
+                gather(1)
+            if a == 4:
+                gather(2)
             part(a)
             quantize(a)
             multiply([a], acc)
         for i in range(6, 8):
             quantize(i)
-        ys = add_bias(0, acc)
+        ys = []
+        for j in range(0, TILES, 2):
+            y = ypool.tile([P, 2, NW], F32, name="y")
+            for u in range(2):
+                nc.vector.tensor_tensor(y[:, u], acc[j + u][:], bias[:, 0:NW], ADD)
+            ys.append(y)
         for i in range(8, 12):
             quantize(i)
-        finish(0, ys)
+        for j in range(0, TILES, 2):
+            y = ys[j // 2]
+            for u in range(2):
+                nc.scalar.activation(y[:, u], y[:, u], GELU)
+            nc.sync.dma_start(out[P * j : P * (j + 2), 0:NW].rearrange("(u p) n -> p u n", u=2), y[:])
         acc = [psum.tile([P, NW], F32, name="acc") for j in range(TILES)]
         for i in range(6, 9):
             multiply([i], acc)
         multiply([9, 10, 11], acc)
-        finish(1, add_bias(1, acc))
+        for j in range(TILES):
+            cuts = [0, NW] if j < TILES - 1 else [0, NW // 2, NW]
+            for lo, hi in zip(cuts, cuts[1:]):
+                z = zpool.tile([P, hi - lo], F32, name="z")
+                nc.vector.tensor_tensor(z[:], acc[j][:, lo:hi], bias[:, NW + lo : NW + hi], ADD)
+                nc.scalar.activation(z[:], z[:], GELU)
+                nc.sync.dma_start(out[P * j : P * (j + 1), NW + lo : NW + hi], z[:])

from contextlib import ExitStack

import concourse.mybir as mybir
from concourse.masks import make_identity

K, M, T, S = 3072, 1024, 2048, 1024
FLOPS = 2 * K * M * S

F32 = mybir.dt.float32
BF16 = mybir.dt.bfloat16
I32 = mybir.dt.int32
U32 = mybir.dt.uint32
U16 = mybir.dt.uint16
U8 = mybir.dt.uint8
FP8X4 = mybir.dt.float8_e4m3fn_x4
FP4X4 = mybir.dt.float4_e2m1fn_x4
GELU = mybir.ActivationFunctionType.Gelu_apprx_tanh
ADD = mybir.AluOpType.add

P = 128
PAIRS = K // 1024
NW = 512
HALVES = M // NW
TILES = S // P
WORD_BYTES = 512 * T
SCALAR_COLUMNS = [512] * 6 + [256] * 6


def tile_list_tab4_tm_gelu_kernel(tc, tab, w, b, offs, out):
    nc = tc.nc
    with ExitStack() as ctx:
        keep = ctx.enter_context(tc.tile_pool(name="keep", bufs=1))
        wpool = ctx.enter_context(tc.tile_pool(name="wpool", bufs=4))
        gpool = ctx.enter_context(tc.tile_pool(name="gpool", bufs=2))
        xpool = ctx.enter_context(tc.tile_pool(name="xpool", bufs=4))
        cpool = ctx.enter_context(tc.tile_pool(name="cpool", bufs=8))
        ypool = ctx.enter_context(tc.tile_pool(name="ypool", bufs=4))
        zpool = ctx.enter_context(tc.tile_pool(name="zpool", bufs=9))
        psum = ctx.enter_context(tc.psum_pool(name="psum", bufs=8))

        offsets = keep.tile([P, S // 16], U16, name="offsets")
        words = [keep.tile([P, T], I32, name=f"words{m}") for m in range(PAIRS)]
        sc = keep.tile([P, PAIRS * T], U8, name="sc", align_bytes=64)
        scg = keep.tile([P, PAIRS * S], U8, name="scg", align_bytes=64)
        sco = keep.tile([P, PAIRS * S], U8, name="sco", align_bytes=64)
        brow = keep.tile([P, P], F32, name="brow")
        ident = keep.tile([P, P], F32, name="ident")
        bcol = keep.tile([P, M // P], F32, name="bcol")
        bias = keep.tile([P, M], F32, name="bias")
        warm = keep.tile([P, 1], F32, name="warm")

        chunk_list = [(half, a) for half in range(HALVES) for a in range(2 * PAIRS)]
        raws = []

        def new_raw():
            raw = wpool.tile([P, 4, NW], F32, name="raw")
            raws.append(raw)
            return raw

        nc.vector.memset(sc[:].bitcast(I32), 0)
        first = [new_raw() for i in range(4)]
        for m in range(1, PAIRS):
            nc.vector.memset(words[m][:, 0:1], 0)
        for raw in first:
            nc.vector.memset(raw[:, 0, 0:1], 0.0)
        nc.gpsimd.memset(brow[:], 0.0)
        nc.gpsimd.memset(warm[:], 0.0)
        make_identity(nc, ident[:])
        nc.gpsimd.memset(sco[:].bitcast(I32), 0)
        nc.scalar.activation(warm[:], warm[:], GELU)

        def load_words(m):
            nc.sync.dma_start(words[m][:], tab[m, 0:WORD_BYTES].bitcast(I32).rearrange("(p t) -> p t", p=P))

        def load_w(i):
            half, a = chunk_list[i]
            raw = raws[i] if i < 4 else new_raw()
            nc.sync.dma_start(raw[:], w[512 * a : 512 * (a + 1), NW * half : NW * (half + 1)].rearrange("(p j) n -> p j n", j=4))

        nc.sync.dma_start(offsets[:], offs)
        load_words(0)
        nc.sync.dma_start(brow[0:8, :], b.rearrange("(m n) -> m n", m=8))
        planes = tab[:, WORD_BYTES : WORD_BYTES + 32 * T].bitcast(I32).rearrange("m (h q r t) -> h q r m t", h=2, q=4, r=4)
        sc_words = sc[:].bitcast(I32).rearrange("p (m t) -> p m t", m=PAIRS)
        for q in range(4):
            nc.sync.dma_start(sc_words[32 * q : 32 * q + 4], planes[0, q])
        odd = tab[:, WORD_BYTES + 16 * T : WORD_BYTES + 32 * T].bitcast(I32).rearrange("m (s t) -> s m t", s=16)
        nc.sync.dma_start(sc_words[4:20], odd)
        load_w(0)
        load_w(1)
        load_words(1)
        load_w(2)
        load_words(2)
        load_w(3)

        tp = psum.tile([P, NW], F32, name="acc")
        nc.tensor.transpose(tp[:, 0:P], brow[:], ident[:])
        nc.scalar.copy(bcol[:], tp[:, 0:8])
        for half in range(HALVES):
            bp = psum.tile([P, NW], F32, name="acc")
            for q in range(4):
                nc.tensor.transpose(bp[:, P * q : P * (q + 1)], bcol[:, 4 * half + q : 4 * half + q + 1].to_broadcast([P, P]), ident[:])
            nc.scalar.copy(bias[:, NW * half : NW * (half + 1)], bp[:])

        def gather_scales(m):
            nc.vector.tensor_copy(scg[:, S * m : S * (m + 1)], sc[:, T * m : T * (m + 1)].indirect(offsets[:]))

        def move_odd_planes(m0, m1):
            for q in range(4):
                nc.scalar.dma_start(
                    sco[32 * q : 32 * q + 4, S * m0 : S * m1].bitcast(I32),
                    scg[4 + 4 * q : 8 + 4 * q, S * m0 : S * m1].bitcast(I32),
                )

        parted = []

        got_of = {}

        def gather(m):
            got = gpool.tile([P, S], U32, name="got")
            nc.vector.tensor_copy(got[:], words[m][:].bitcast(U32).indirect(offsets[:]))
            got_of[m] = got

        def part(a):
            m, h = divmod(a, 2)
            pt = keep.tile([P, 2 * S], U8, name=f"parted{a}", align_bytes=64)
            nc.vector.tensor_copy(pt[:].bitcast(U16), got_of[m][:].bitcast(U16).rearrange("p (t h) -> p h t", h=2)[:, h, :])
            parted.append(pt)

        quantized = []

        def quantize(i):
            raw = raws[i]
            x = xpool.tile([P, 4 * NW], BF16, name="x", align_bytes=64)
            cut = SCALAR_COLUMNS[i]
            for engine, lo, hi in ((nc.scalar.copy, 0, cut), (nc.vector.tensor_copy, cut, NW)):
                if lo < hi:
                    engine(
                        x[:, 4 * lo : 4 * hi].rearrange("p (c i t) -> p c t i", i=4, t=4),
                        raw[:, :, lo:hi].rearrange("p t (c i) -> p c t i", i=4),
                    )
            codes = cpool.tile([P, NW], U32, name="codes", align_bytes=64)
            scales = cpool.tile([P, NW], U8, name="scales", align_bytes=64)
            nc.vector.quantize_mx(out=codes[:].bitcast(FP8X4), scales=scales[:], in_=x[:])
            quantized.append((codes, scales))
            if i + 4 < len(chunk_list):
                load_w(i + 4)

        def multiply(chunks, acc):
            for j in range(TILES):
                for i in chunks:
                    a = i % 6
                    m, h = divmod(a, 2)
                    codes, scales = quantized[i]
                    plane = (scg, sco)[h]
                    nc.tensor.matmul_mx(
                        out=acc[j][:],
                        lhsT=parted[a][:, 2 * P * j : 2 * P * (j + 1)].bitcast(FP4X4),
                        lhsT_scale=plane[:, S * m + P * j : S * m + P * (j + 1)],
                        rhs=codes[:].bitcast(FP8X4),
                        rhs_scale=scales[:],
                        start=(a == 0),
                        stop=(a == 5),
                    )

        def add_bias(half, acc):
            ys = []
            for j in range(TILES):
                y = ypool.tile([P, NW], F32, name="y")
                nc.vector.tensor_tensor(y[:], acc[j][:], bias[:, NW * half : NW * (half + 1)], ADD)
                ys.append(y)
            return ys

        acc = [psum.tile([P, NW], F32, name="acc") for j in range(TILES)]
        gather(0)
        gather_scales(0)
        move_odd_planes(0, 1)
        for a in range(6):
            if a == 2:
                gather_scales(1)
                gather_scales(2)
                move_odd_planes(1, 3)
                gather(1)
            if a == 4:
                gather(2)
            part(a)
            quantize(a)
            multiply([a], acc)
        for i in range(6, 8):
            quantize(i)
        ys = []
        for j in range(0, TILES, 2):
            y = ypool.tile([P, 2, NW], F32, name="y")
            for u in range(2):
                nc.vector.tensor_tensor(y[:, u], acc[j + u][:], bias[:, 0:NW], ADD)
            ys.append(y)
        for i in range(8, 12):
            quantize(i)
        for j in range(0, TILES, 2):
            y = ys[j // 2]
            for u in range(2):
                nc.scalar.activation(y[:, u], y[:, u], GELU)
            nc.sync.dma_start(out[P * j : P * (j + 2), 0:NW].rearrange("(u p) n -> p u n", u=2), y[:])
        acc = [psum.tile([P, NW], F32, name="acc") for j in range(TILES)]
        for i in range(6, 9):
            multiply([i], acc)
        multiply([9, 10, 11], acc)
        for j in range(TILES):
            cuts = [0, NW] if j < TILES - 1 else [0, NW // 2, NW]
            for lo, hi in zip(cuts, cuts[1:]):
                z = zpool.tile([P, hi - lo], F32, name="z")
                nc.vector.tensor_tensor(z[:], acc[j][:, lo:hi], bias[:, NW + lo : NW + hi], ADD)
                nc.scalar.activation(z[:], z[:], GELU)
                nc.sync.dma_start(out[P * j : P * (j + 1), NW + lo : NW + hi], z[:])
